import numpy as np
import ml_dtypes


def mxq(x, axis, fmt="e4m3"):
    dtype, down = {"e4m3": (ml_dtypes.float8_e4m3fn, 7), "e5m2": (ml_dtypes.float8_e5m2, 14)}[fmt]
    v = np.moveaxis(np.asarray(x, np.float32).astype(ml_dtypes.bfloat16).astype(np.float64), axis, -1)
    blocks = v.reshape(v.shape[:-1] + (-1, 32))
    amax = np.abs(blocks).max(-1, keepdims=True)
    byte = np.maximum(np.where(amax > 0, np.frexp(amax)[1] - 1 + 127, 0) - down, 1)
    scale = np.exp2(byte - 127.0)
    codes = (blocks / scale).astype(np.float32).astype(dtype).astype(np.float64)
    return np.moveaxis((codes * scale).reshape(v.shape), -1, axis)


WIDE = False


def mx_kscale(k):
    if not WIDE:
        return np.ones(k)
    levels = np.array([10, -10, 5, -5, 0])
    if k % 512:
        return np.exp2(np.random.permutation(np.resize(levels, k // 32))).repeat(32)
    a = np.empty((k // 512, 16))
    for p in range(k // 512):
        a[p, :8] = np.random.permutation(np.resize(levels, 8))
        for g in range(8):
            far = levels[np.abs(levels - a[p, g]) >= 10]
            a[p, g + 8] = far[np.random.randint(len(far))]
    return np.exp2(a.ravel()).repeat(32)


def f64(x):
    return np.asarray(x).astype(np.float64)


def striped(idx):
    return np.tile(idx.reshape(-1, 16).T, (8, 1)).astype(np.uint16)


def unstriped(offs):
    return offs[:16].T.reshape(-1).astype(np.int64)


E2M1 = np.array([0.0, 0.5, 1.0, 1.5, 2.0, 3.0, 4.0, 6.0, -0.0, -0.5, -1.0, -1.5, -2.0, -3.0, -4.0, -6.0])


def pack_weight(w, fmt):
    k, n = w.shape
    w = f64(np.asarray(w, np.float32).astype(ml_dtypes.bfloat16)).reshape(k // 32, 32, n)
    amax = np.abs(w).max(1)
    if fmt == "e4m3":
        byte = np.frexp(amax)[1] - 1 + 127 - 7
    else:
        mant, ex = np.frexp(amax / 6.0)
        byte = np.where(mant > 0.5, ex, ex - 1) + 127
    byte = np.clip(np.where(amax > 0, byte, 1), 1, 254)
    scaled = (w * np.exp2(127.0 - byte)[:, None, :]).reshape(k, n).astype(np.float32)
    by_word = np.ascontiguousarray(scaled.reshape(k // 512, 128, 4, n).transpose(0, 1, 3, 2))
    if fmt == "e4m3":
        words = by_word.astype(ml_dtypes.float8_e4m3fn).view(np.uint8)
    else:
        c = by_word.astype(ml_dtypes.float4_e2m1fn).view(np.uint8) & 0xF
        words = (c[..., 0::2] | (c[..., 1::2] << 4)).reshape(k // 512, 128, 2 * n)
    return np.ascontiguousarray(words), np.ascontiguousarray(byte.astype(np.uint8).reshape(k // 512, 16, n))


def unpack_weight(words, scales, fmt):
    g, _, n = scales.shape
    words = np.ascontiguousarray(words).reshape(g, 128, n, -1)
    if fmt == "e4m3":
        vals = words.view(ml_dtypes.float8_e4m3fn).astype(np.float64)
    else:
        nib = np.empty((g, 128, n, 4), np.uint8)
        nib[..., 0::2] = words & 0xF
        nib[..., 1::2] = words >> 4
        vals = E2M1[nib]
    vals = vals * np.repeat(np.exp2(scales.astype(np.float64) - 127.0), 8, axis=1)[..., None]
    return vals.transpose(0, 1, 3, 2).reshape(g * 512, n)


def gelu(v):
    return 0.5 * v * (1.0 + np.tanh(np.sqrt(2.0 / np.pi) * (v + 0.044715 * v**3)))


def striped8(idx):
    return np.concatenate([v.reshape(-1, 16).T for v in idx]).astype(np.uint16)


def unstriped8(offs):
    return np.stack([offs[16 * g:16 * g + 16].T.reshape(-1) for g in range(8)]).astype(np.int64)


def runs(v, idx8):
    k = np.arange(v.shape[0])
    return v[k[:, None], idx8[k % 512 // 64]]


K, T, S, P, H, N = 1024, 2048, 1024, 512, 512, 512


def setup_inputs():
    n = np.random.standard_normal
    s = mx_kscale(K)[:, None]
    u = mx_kscale(H)[:, None]
    d = {}
    d["tab_words"], d["tab_scales"] = pack_weight(n((K, T)) * s, "e4m3")
    d["offs"] = striped8(np.stack([np.random.permutation(T)[:S] for _ in range(8)]))
    d["wa"] = (1.3 * n((K, H)) / K**0.5 / s).astype(np.float32)
    d["ba"] = (0.5 * n(H)).astype(np.float32)
    d["ga"] = (1.3 * np.exp(0.3 * n(H)) * u[:, 0]).astype(np.float32)
    d["wd_words"], d["wd_scales"] = pack_weight(n((K, H)) / K**0.5 / s * u.T, "e2m1")
    d["pos1"] = striped(np.random.permutation(S)[:P])
    d["pos2"] = striped(np.random.permutation(S)[:P])
    d["we"] = (1.2 * n((H, N)) / H**0.5 / u).astype(np.float32)
    d["be"] = (0.5 * n(N)).astype(np.float32)
    return d


def reference(tab_words, tab_scales, offs, wa, ba, ga, wd_words, wd_scales, pos1, pos2, we, be):
    v = runs(unpack_weight(tab_words, tab_scales, "e4m3"), unstriped8(offs))
    ya = mxq(f64(wa), 0, "e4m3").T @ v
    a = f64(ga)[:, None] * np.tanh(ya + f64(ba)[:, None])
    b = unpack_weight(wd_words, wd_scales, "e2m1").T @ v
    z = a[:, unstriped(pos1)] - b[:, unstriped(pos2)]
    y = mxq(f64(we), 0, "e4m3").T @ mxq(z, 0, "e4m3")
    y = y + f64(be)[:, None]
    return y / (1.0 + np.exp(-y))

@@ -1,0 +1,251 @@
+from contextlib import ExitStack
+
+import concourse.mybir as mybir
+from concourse.masks import make_identity
+
+K, T, S, M, H, N = 1024, 2048, 1024, 512, 512, 512
+FLOPS = 2 * (2 * K * H * S + H * N * M)
+
+F32 = mybir.dt.float32
+BF16 = mybir.dt.bfloat16
+I32 = mybir.dt.int32
+U32 = mybir.dt.uint32
+U16 = mybir.dt.uint16
+U8 = mybir.dt.uint8
+FP8X4 = mybir.dt.float8_e4m3fn_x4
+FP4X4 = mybir.dt.float4_e2m1fn_x4
+ACT = mybir.ActivationFunctionType
+ALU = mybir.AluOpType
+
+P = 128
+PASSES = 2
+SLOTS = 4
+BANK = 512
+HALVES = S // BANK
+CHUNKS = (256, 128, 128)
+
+
+def tile_list_dispense_stroke_correction_kernel(
+    tc, tab_words, tab_scales, offs, wa, ba, ga, wd_words, wd_scales, pos1, pos2, we, be, out
+):
+    nc = tc.nc
+    with ExitStack() as ctx:
+        lists = ctx.enter_context(tc.tile_pool(name="lists", bufs=1))
+        keep = ctx.enter_context(tc.tile_pool(name="keep", bufs=1))
+        stage = ctx.enter_context(tc.tile_pool(name="stage", bufs=1))
+        psum = ctx.enter_context(tc.psum_pool(name="psum", bufs=1))
+
+        def sb(shape, dtype, name, tag=None):
+            return keep.tile(shape, dtype, name=name, tag=tag or name, align_bytes=64)
+
+        def bank(i):
+            return psum.tile([P, BANK], F32, name="bank", tag="bank%d" % (i % 8))
+
+        offs_sb = lists.tile([P, S // 16], U16, name="offs_sb")
+        pos1_sb = lists.tile([P, M // 16], U16, name="pos1_sb")
+        pos2_sb = lists.tile([P, M // 16], U16, name="pos2_sb")
+        nc.sync.dma_start(offs_sb[:], offs)
+
+        scale_win = sb([P, T // 4], I32, "scale_win")
+        for a in range(PASSES):
+            for jj in range(2):
+                nc.sync.dma_start(
+                    scale_win[2 * a + jj : P : 4, :],
+                    tab_scales[a, jj:16:2, :].bitcast(I32).unsqueeze(1).broadcast_to([8, 4, T // 4]),
+                )
+        wd_raw = stage.tile([P, PASSES, H // 2], I32, name="wd_raw", offset=8192)
+        nc.sync.dma_start(wd_raw[:], wd_words.rearrange("a p c -> p a c").bitcast(I32))
+        word_win = []
+        for a in range(PASSES):
+            win = sb([P, T], I32, "word_win%d" % a)
+            nc.sync.dma_start(win[:], tab_words[a].rearrange("p t i -> p (t i)").bitcast(I32))
+            word_win.append(win)
+        nc.sync.dma_start(pos1_sb[:], pos1)
+        nc.sync.dma_start(pos2_sb[:], pos2)
+
+        warm_in = sb([P, 8], F32, "warm_in")
+        warm_out = sb([P, 8], F32, "warm_out")
+        nc.vector.memset(warm_in[:], 0.0)
+        nc.scalar.activation(warm_out[:], warm_in[:], ACT.Silu)
+
+        wds_raw = sb([P, PASSES, H // 4], I32, "wds_raw")
+        nc.gpsimd.memset(wds_raw[:], 0)
+        plane_tiles = []
+        for a in range(PASSES):
+            plane = sb([P, S // 4], I32, "plane%d" % a)
+            plane_tiles.append(plane)
+        nc.vector.memset(plane_tiles[1][:], 0)
+        vec_rows = sb([P, P], F32, "vec_rows")
+        nc.vector.memset(vec_rows[:], 0.0)
+        for r in range(4):
+            nc.gpsimd.dma_start(
+                wds_raw[r:P:32, :, :],
+                wd_scales[:, r:16:4, :].rearrange("a d c -> d a c").bitcast(I32),
+            )
+        for row0, vec in ((0, ba), (4, ga)):
+            nc.gpsimd.dma_start(
+                vec_rows[row0 : row0 + 4, :].rearrange("t (b i) -> t b i", i=8),
+                vec.rearrange("(b t i) -> t b i", t=4, i=8),
+            )
+        nc.gpsimd.dma_start(vec_rows[8:12, :], be.rearrange("(j p) -> j p", p=P))
+        ident = sb([P, P], F32, "ident")
+        make_identity(nc, ident[:])
+
+        picked_scales = sb([P, S], U8, "picked_scales")
+        nc.vector.tensor_copy(picked_scales[:], scale_win[:].bitcast(U8).indirect(offs_sb[:]))
+        picked_i32 = picked_scales[:].bitcast(I32)
+        nc.vector.tensor_copy(plane_tiles[0][:], picked_i32)
+        for a in range(PASSES):
+            for r in range(4):
+                src = 16 * (r // 2) + 2 * a + r % 2
+                if src != r:
+                    nc.scalar.dma_start(plane_tiles[a][r:P:32, :], picked_i32[src:P:32, :])
+        planes = [plane[:].bitcast(U8) for plane in plane_tiles]
+
+        wd_sb = sb([P, PASSES * H // 2], I32, "wd_sb")
+        nc.vector.tensor_copy(
+            wd_sb[:].rearrange("p (a t b w) -> p a t b w", a=PASSES, t=4, w=4),
+            wd_raw[:].rearrange("p a (b t w) -> p a t b w", t=4, w=4),
+        )
+        picked = []
+        for a in range(PASSES):
+            row = []
+            for h in range(HALVES):
+                g = sb([P, BANK], U32, "picked%d%d" % (a, h))
+                nc.vector.tensor_copy(g[:], word_win[a][:].bitcast(U32).indirect(offs_sb[:, 32 * h : 32 * (h + 1)]))
+                row.append(g)
+            picked.append(row)
+            if a == 0:
+                wds_sb = sb([P, PASSES * H // 4], I32, "wds_sb")
+                nc.vector.tensor_copy(
+                    wds_sb[:].rearrange("p (a t b w) -> p a t b w", a=PASSES, t=4, w=2),
+                    wds_raw[:].rearrange("p a (b t w) -> p a t b w", t=4, w=2),
+                )
+
+        wa_raw = []
+        for a in range(PASSES):
+            raw = stage.tile([P, SLOTS, H], F32, name="wa_raw%d" % a, offset=8192 * a)
+            nc.sync.dma_start(raw[:], wa[512 * a : 512 * (a + 1), :].rearrange("(p j) c -> p j c", j=4))
+            wa_raw.append(raw)
+
+        wd_u8 = wd_sb[:].bitcast(U8)
+        wds_u8 = wds_sb[:].bitcast(U8)
+        b_ps = {}
+        for t0 in (0, 2):
+            for a, h in ((0, 0), (0, 1), (1, 0), (1, 1)):
+                for t in (t0, t0 + 1):
+                    if a == 0:
+                        b_ps[(t, h)] = bank(SLOTS * h + t)
+                    c0 = a * H + t * P
+                    nc.tensor.matmul_mx(
+                        out=b_ps[(t, h)][:],
+                        lhsT=wd_u8[:, 2 * c0 : 2 * (c0 + P)].bitcast(FP4X4),
+                        lhsT_scale=wds_u8[:, c0 : c0 + P],
+                        rhs=picked[a][h][:].bitcast(FP8X4),
+                        rhs_scale=planes[a][:, BANK * h : BANK * (h + 1)],
+                        start=(a == 0),
+                        stop=(a == PASSES - 1),
+                    )
+
+        wa_codes, wa_sc = [], []
+        for a in range(PASSES):
+            wa_bf = sb([P, SLOTS * H], BF16, "wa_bf%d" % a)
+            dst = wa_bf[:].rearrange("p (t b i j) -> p t b i j", t=4, i=8, j=4)
+            src = wa_raw[a][:].rearrange("p j (b t i) -> p t b i j", t=4, i=8)
+            if a == 0:
+                nc.scalar.copy(dst[:, 0:2], src[:, 0:2])
+                nc.vector.tensor_copy(dst[:, 2:4], src[:, 2:4])
+            else:
+                nc.vector.tensor_copy(dst, src)
+            codes = sb([P, H], U32, "wa_codes%d" % a)
+            sc = sb([P, H], U8, "wa_sc%d" % a)
+            nc.vector.quantize_mx(out=codes[:].bitcast(FP8X4), scales=sc[:], in_=wa_bf[:])
+            wa_codes.append(codes)
+            wa_sc.append(sc)
+
+        we_raw = stage.tile([P, SLOTS, N], F32, name="we_raw", offset=0)
+        we_rows = we.rearrange("(b t i) n -> t b i n", t=4, i=8)
+        for t in range(SLOTS):
+            nc.sync.dma_start(we_raw[:, t, :], we_rows[t])
+
+        b_pick = []
+        for t in range(SLOTS):
+            b_sb = sb([P, S], F32, "b_sb%d" % t)
+            for h in range(HALVES):
+                nc.scalar.copy(b_sb[:, BANK * h : BANK * (h + 1)], b_ps[(t, h)][:])
+            g2 = sb([P, M], F32, "b_pick%d" % t)
+            nc.vector.tensor_copy(g2[:], b_sb[:].indirect(pos2_sb[:]))
+            b_pick.append(g2)
+
+        vec_ps = bank(1)
+        nc.tensor.transpose(vec_ps[:, 0:P], vec_rows[:], ident[:])
+        vecs = sb([P, 16], F32, "vecs")
+        nc.scalar.copy(vecs[:], vec_ps[:, 0:16])
+
+        a_sb = []
+        for t in range(SLOTS):
+            th = sb([P, S], F32, "a_sb%d" % t)
+            for h in range(HALVES):
+                ps = bank(SLOTS * h + t)
+                for a in range(PASSES):
+                    nc.tensor.matmul_mx(
+                        out=ps[:],
+                        lhsT=wa_codes[a][:, t * P : (t + 1) * P].bitcast(FP8X4),
+                        lhsT_scale=wa_sc[a][:, t * P : (t + 1) * P],
+                        rhs=picked[a][h][:].bitcast(FP8X4),
+                        rhs_scale=planes[a][:, BANK * h : BANK * (h + 1)],
+                        start=(a == 0),
+                        stop=(a == PASSES - 1),
+                    )
+                nc.scalar.activation(th[:, BANK * h : BANK * (h + 1)], ps[:], ACT.Tanh, bias=vecs[:, t : t + 1])
+            a_sb.append(th)
+
+        we_bf = sb([P, N, SLOTS], BF16, "we_bf", "wa_codes1")
+        nc.scalar.copy(we_bf[:], we_raw[:].rearrange("p t n -> p n t"))
+        we_codes = sb([P, N], U32, "we_codes")
+        we_sc = sb([P, N], U8, "we_sc")
+
+        out_rows = out.rearrange("(j p) m -> p j m", p=P)
+        m0 = 0
+        next_bank = 0
+        for c, width in enumerate(CHUNKS):
+            z_rows = sb([P, SLOTS, width], BF16, "z_rows%d" % c)
+            for t in range(SLOTS):
+                g1 = sb([P, width], F32, "a_pick%d%d" % (c, t))
+                nc.vector.tensor_copy(g1[:], a_sb[t][:].indirect(pos1_sb[:, m0 // 16 : (m0 + width) // 16]))
+                nc.vector.scalar_tensor_tensor(
+                    z_rows[:, t, :], g1[:], vecs[:, 4 + t : 5 + t], b_pick[t][:, m0 : m0 + width],
+                    ALU.mult, ALU.subtract,
+                )
+            if c == 0:
+                nc.vector.quantize_mx(
+                    out=we_codes[:].bitcast(FP8X4), scales=we_sc[:], in_=we_bf[:].rearrange("p n t -> p (n t)")
+                )
+            z_bf = sb([P, width, SLOTS], BF16, "z_bf%d" % c)
+            if c < len(CHUNKS) - 1:
+                nc.scalar.copy(z_bf[:], z_rows[:].rearrange("p t m -> p m t"))
+            else:
+                nc.vector.tensor_copy(z_bf[:], z_rows[:].rearrange("p t m -> p m t"))
+            z_codes = sb([P, width], U32, "z_codes%d" % c)
+            z_sc = sb([P, width], U8, "z_sc%d" % c)
+            nc.vector.quantize_mx(
+                out=z_codes[:].bitcast(FP8X4), scales=z_sc[:], in_=z_bf[:].rearrange("p m t -> p (m t)")
+            )
+            for jp in range(2):
+                y_sb = sb([P, 2, width], F32, "y_sb%d%d" % (c, jp))
+                for jj in range(2):
+                    j = 2 * jp + jj
+                    ps = bank(next_bank)
+                    next_bank = next_bank + 1
+                    nc.tensor.matmul_mx(
+                        out=ps[:, 0:width],
+                        lhsT=we_codes[:, j * P : (j + 1) * P].bitcast(FP8X4),
+                        lhsT_scale=we_sc[:, j * P : (j + 1) * P],
+                        rhs=z_codes[:].bitcast(FP8X4),
+                        rhs_scale=z_sc[:],
+                        start=True,
+                        stop=True,
+                    )
+                    nc.scalar.activation(y_sb[:, jj, :], ps[:, 0:width], ACT.Silu, bias=vecs[:, 8 + j : 9 + j])
+                nc.sync.dma_start(out_rows[:, 2 * jp : 2 * jp + 2, m0 : m0 + width], y_sb[:])
+            m0 = m0 + width

@@ -46,66 +46,63 @@ def tile_list_dispense_stroke_correction_kernel(
         pos2_sb = lists.tile([P, M // 16], U16, name="pos2_sb")
         nc.sync.dma_start(offs_sb[:], offs)
 
-        scale_win = sb([P, T // 4], I32, "scale_win")
-        for a in range(PASSES):
-            for jj in range(2):
-                nc.sync.dma_start(
-                    scale_win[2 * a + jj : P : 4, :],
-                    tab_scales[a, jj:16:2, :].bitcast(I32).unsqueeze(1).broadcast_to([8, 4, T // 4]),
-                )
-        wd_raw = stage.tile([P, PASSES, H // 2], I32, name="wd_raw", offset=8192)
+        nc.sync.dma_start(pos1_sb[:], pos1)
+        nc.sync.dma_start(pos2_sb[:], pos2)
+        scale_win = stage.tile([P, T // 4], I32, name="scale_win", offset=7168)
+        nc.vector.memset(scale_win[:], 0)
+        nc.sync.dma_start(scale_win[0:P:4, :], tab_scales.rearrange("a q c -> q a c").bitcast(I32))
+        wd_raw = sb([P, PASSES, H // 2], I32, "wd_raw")
         nc.sync.dma_start(wd_raw[:], wd_words.rearrange("a p c -> p a c").bitcast(I32))
+        wds_raw = sb([P, PASSES, H // 4], I32, "wds_raw")
+        nc.gpsimd.memset(wds_raw[:], 0)
         word_win = []
         for a in range(PASSES):
             win = sb([P, T], I32, "word_win%d" % a)
             nc.sync.dma_start(win[:], tab_words[a].rearrange("p t i -> p (t i)").bitcast(I32))
             word_win.append(win)
-        nc.sync.dma_start(pos1_sb[:], pos1)
-        nc.sync.dma_start(pos2_sb[:], pos2)
+            if a == 0:
+                for d in range(4):
+                    nc.sync.dma_start(
+                        wds_raw[32 * d : 32 * d + 4, :, :],
+                        wd_scales[:, 4 * d : 4 * d + 4, :].rearrange("a r c -> r a c").bitcast(I32),
+                    )
 
         warm_in = sb([P, 8], F32, "warm_in")
         warm_out = sb([P, 8], F32, "warm_out")
         nc.vector.memset(warm_in[:], 0.0)
         nc.scalar.activation(warm_out[:], warm_in[:], ACT.Silu)
 
-        wds_raw = sb([P, PASSES, H // 4], I32, "wds_raw")
-        nc.gpsimd.memset(wds_raw[:], 0)
         plane_tiles = []
         for a in range(PASSES):
             plane = sb([P, S // 4], I32, "plane%d" % a)
+            nc.gpsimd.memset(plane[:], 0)
             plane_tiles.append(plane)
-        nc.vector.memset(plane_tiles[1][:], 0)
-        vec_rows = sb([P, P], F32, "vec_rows")
-        nc.vector.memset(vec_rows[:], 0.0)
-        for r in range(4):
-            nc.gpsimd.dma_start(
-                wds_raw[r:P:32, :, :],
-                wd_scales[:, r:16:4, :].rearrange("a d c -> d a c").bitcast(I32),
-            )
-        for row0, vec in ((0, ba), (4, ga)):
-            nc.gpsimd.dma_start(
-                vec_rows[row0 : row0 + 4, :].rearrange("t (b i) -> t b i", i=8),
-                vec.rearrange("(b t i) -> t b i", t=4, i=8),
-            )
-        nc.gpsimd.dma_start(vec_rows[8:12, :], be.rearrange("(j p) -> j p", p=P))
         ident = sb([P, P], F32, "ident")
         make_identity(nc, ident[:])
 
         picked_scales = sb([P, S], U8, "picked_scales")
         nc.vector.tensor_copy(picked_scales[:], scale_win[:].bitcast(U8).indirect(offs_sb[:]))
         picked_i32 = picked_scales[:].bitcast(I32)
-        nc.vector.tensor_copy(plane_tiles[0][:], picked_i32)
+        wa_raw = []
         for a in range(PASSES):
-            for r in range(4):
-                src = 16 * (r // 2) + 2 * a + r % 2
-                if src != r:
-                    nc.scalar.dma_start(plane_tiles[a][r:P:32, :], picked_i32[src:P:32, :])
+            for d in range(4):
+                nc.sync.dma_start(
+                    plane_tiles[a][32 * d : 32 * d + 4, :], picked_i32[32 * d + 4 * a : 32 * d + 32 : 8, :]
+                )
+            raw = stage.tile([P, SLOTS, H], F32, name="wa_raw%d" % a, offset=8192 * a)
+            nc.sync.dma_start(raw[:], wa[512 * a : 512 * (a + 1), :].rearrange("(p j) c -> p j c", j=4))
+            wa_raw.append(raw)
         planes = [plane[:].bitcast(U8) for plane in plane_tiles]
 
         wd_sb = sb([P, PASSES * H // 2], I32, "wd_sb")
         nc.vector.tensor_copy(
             wd_sb[:].rearrange("p (a t b w) -> p a t b w", a=PASSES, t=4, w=4),
             wd_raw[:].rearrange("p a (b t w) -> p a t b w", t=4, w=4),
+        )
+        wds_sb = sb([P, PASSES * H // 4], I32, "wds_sb")
+        nc.vector.tensor_copy(
+            wds_sb[:].rearrange("p (a t b w) -> p a t b w", a=PASSES, t=4, w=2),
+            wds_raw[:].rearrange("p a (b t w) -> p a t b w", t=4, w=2),
         )
         picked = []
         for a in range(PASSES):
@@ -115,25 +112,23 @@ def tile_list_dispense_stroke_correction_kernel(
                 nc.vector.tensor_copy(g[:], word_win[a][:].bitcast(U32).indirect(offs_sb[:, 32 * h : 32 * (h + 1)]))
                 row.append(g)
             picked.append(row)
-            if a == 0:
-                wds_sb = sb([P, PASSES * H // 4], I32, "wds_sb")
-                nc.vector.tensor_copy(
-                    wds_sb[:].rearrange("p (a t b w) -> p a t b w", a=PASSES, t=4, w=2),
-                    wds_raw[:].rearrange("p a (b t w) -> p a t b w", t=4, w=2),
-                )
 
-        wa_raw = []
-        for a in range(PASSES):
-            raw = stage.tile([P, SLOTS, H], F32, name="wa_raw%d" % a, offset=8192 * a)
-            nc.sync.dma_start(raw[:], wa[512 * a : 512 * (a + 1), :].rearrange("(p j) c -> p j c", j=4))
-            wa_raw.append(raw)
+
+        vec_rows = sb([P, P], F32, "vec_rows", "wds_raw")
+        nc.gpsimd.memset(vec_rows[:], 0.0)
+        for row0, vec in ((0, ba), (4, ga)):
+            nc.sync.dma_start(
+                vec_rows[row0 : row0 + 4, :].rearrange("t (b i) -> t b i", i=8),
+                vec.rearrange("(b t i) -> t b i", t=4, i=8),
+            )
+        nc.sync.dma_start(vec_rows[8:12, :], be.rearrange("(j p) -> j p", p=P))
 
         wd_u8 = wd_sb[:].bitcast(U8)
         wds_u8 = wds_sb[:].bitcast(U8)
         b_ps = {}
-        for t0 in (0, 2):
-            for a, h in ((0, 0), (0, 1), (1, 0), (1, 1)):
-                for t in (t0, t0 + 1):
+        for t in range(SLOTS):
+            for a in range(PASSES):
+                for h in range(HALVES):
                     if a == 0:
                         b_ps[(t, h)] = bank(SLOTS * h + t)
                     c0 = a * H + t * P
@@ -154,9 +149,10 @@ def tile_list_dispense_stroke_correction_kernel(
             src = wa_raw[a][:].rearrange("p j (b t i) -> p t b i j", t=4, i=8)
             if a == 0:
                 nc.scalar.copy(dst[:, 0:2], src[:, 0:2])
-                nc.vector.tensor_copy(dst[:, 2:4], src[:, 2:4])
             else:
-                nc.vector.tensor_copy(dst, src)
+                nc.scalar.copy(dst[:, 0], src[:, 0])
+                nc.vector.tensor_copy(dst[:, 1], src[:, 1])
+            nc.vector.tensor_copy(dst[:, 2:4], src[:, 2:4])
             codes = sb([P, H], U32, "wa_codes%d" % a)
             sc = sb([P, H], U8, "wa_sc%d" % a)
             nc.vector.quantize_mx(out=codes[:].bitcast(FP8X4), scales=sc[:], in_=wa_bf[:])
@@ -170,10 +166,16 @@ def tile_list_dispense_stroke_correction_kernel(
 
         b_pick = []
         for t in range(SLOTS):
-            b_sb = sb([P, S], F32, "b_sb%d" % t)
+            if t < 2:
+                b_sb = sb([P, S], F32, "b_sb%d" % t)
+            else:
+                b_sb = stage.tile([P, S], F32, name="b_sb%d" % t, offset=10240 + 4096 * (t - 2))
             for h in range(HALVES):
                 nc.scalar.copy(b_sb[:, BANK * h : BANK * (h + 1)], b_ps[(t, h)][:])
-            g2 = sb([P, M], F32, "b_pick%d" % t)
+            if t == 1:
+                g2 = stage.tile([P, M], F32, name="b_pick%d" % t, offset=8192)
+            else:
+                g2 = sb([P, M], F32, "b_pick%d" % t)
             nc.vector.tensor_copy(g2[:], b_sb[:].indirect(pos2_sb[:]))
             b_pick.append(g2)
 
@@ -200,43 +202,58 @@ def tile_list_dispense_stroke_correction_kernel(
                 nc.scalar.activation(th[:, BANK * h : BANK * (h + 1)], ps[:], ACT.Tanh, bias=vecs[:, t : t + 1])
             a_sb.append(th)
 
-        we_bf = sb([P, N, SLOTS], BF16, "we_bf", "wa_codes1")
-        nc.scalar.copy(we_bf[:], we_raw[:].rearrange("p t n -> p n t"))
+        we_bf = sb([P, N, SLOTS], BF16, "we_bf")
+        for j in range(4):
+            nc.gpsimd.tensor_scalar(
+                we_bf[:, j * P : (j + 1) * P, :],
+                we_raw[:, :, j * P : (j + 1) * P].rearrange("p t n -> p n t"),
+                1.0, 0.0, ALU.mult, ALU.add,
+            )
         we_codes = sb([P, N], U32, "we_codes")
         we_sc = sb([P, N], U8, "we_sc")
 
         out_rows = out.rearrange("(j p) m -> p j m", p=P)
-        m0 = 0
-        next_bank = 0
-        for c, width in enumerate(CHUNKS):
-            z_rows = sb([P, SLOTS, width], BF16, "z_rows%d" % c)
-            for t in range(SLOTS):
-                g1 = sb([P, width], F32, "a_pick%d%d" % (c, t))
-                nc.vector.tensor_copy(g1[:], a_sb[t][:].indirect(pos1_sb[:, m0 // 16 : (m0 + width) // 16]))
-                nc.vector.scalar_tensor_tensor(
-                    z_rows[:, t, :], g1[:], vecs[:, 4 + t : 5 + t], b_pick[t][:, m0 : m0 + width],
-                    ALU.mult, ALU.subtract,
-                )
-            if c == 0:
-                nc.vector.quantize_mx(
-                    out=we_codes[:].bitcast(FP8X4), scales=we_sc[:], in_=we_bf[:].rearrange("p n t -> p (n t)")
-                )
-            z_bf = sb([P, width, SLOTS], BF16, "z_bf%d" % c)
+        starts = [sum(CHUNKS[:c]) for c in range(len(CHUNKS))]
+        steps = [(c, t) for c in range(len(CHUNKS)) for t in range(SLOTS)]
+        z_rows = [sb([P, SLOTS, width], BF16, "z_rows%d" % c) for c, width in enumerate(CHUNKS)]
+        a_pick = {}
+
+        def pick(n):
+            c, t = steps[n]
+            m0, width = starts[c], CHUNKS[c]
+            tag = "z_bf%d" % (c - 1) if c > 0 and t == SLOTS - 1 else "a_pick%d" % (n % 3)
+            a_pick[n] = sb([P, width], F32, "a_pick%d" % n, tag)
+            nc.vector.tensor_copy(a_pick[n][:], a_sb[t][:].indirect(pos1_sb[:, m0 // 16 : (m0 + width) // 16]))
+
+        def combine(n):
+            c, t = steps[n]
+            m0, width = starts[c], CHUNKS[c]
+            nc.vector.scalar_tensor_tensor(
+                z_rows[c][:, t, :], a_pick[n][:], vecs[:, 4 + t : 5 + t], b_pick[t][:, m0 : m0 + width],
+                ALU.mult, ALU.subtract,
+            )
+
+        z_bf = {}
+
+        def weave(c):
+            z_bf[c] = sb([P, CHUNKS[c], SLOTS], BF16, "z_bf%d" % c)
             if c < len(CHUNKS) - 1:
-                nc.scalar.copy(z_bf[:], z_rows[:].rearrange("p t m -> p m t"))
+                nc.scalar.copy(z_bf[c][:], z_rows[c][:].rearrange("p t m -> p m t"))
             else:
-                nc.vector.tensor_copy(z_bf[:], z_rows[:].rearrange("p t m -> p m t"))
+                nc.vector.tensor_copy(z_bf[c][:], z_rows[c][:].rearrange("p t m -> p m t"))
+
+        def finish(c):
+            m0, width = starts[c], CHUNKS[c]
             z_codes = sb([P, width], U32, "z_codes%d" % c)
             z_sc = sb([P, width], U8, "z_sc%d" % c)
             nc.vector.quantize_mx(
-                out=z_codes[:].bitcast(FP8X4), scales=z_sc[:], in_=z_bf[:].rearrange("p m t -> p (m t)")
+                out=z_codes[:].bitcast(FP8X4), scales=z_sc[:], in_=z_bf[c][:].rearrange("p m t -> p (m t)")
             )
             for jp in range(2):
                 y_sb = sb([P, 2, width], F32, "y_sb%d%d" % (c, jp))
                 for jj in range(2):
                     j = 2 * jp + jj
-                    ps = bank(next_bank)
-                    next_bank = next_bank + 1
+                    ps = bank(4 * c + j)
                     nc.tensor.matmul_mx(
                         out=ps[:, 0:width],
                         lhsT=we_codes[:, j * P : (j + 1) * P].bitcast(FP8X4),
@@ -248,4 +265,18 @@ def tile_list_dispense_stroke_correction_kernel(
                     )
                     nc.scalar.activation(y_sb[:, jj, :], ps[:, 0:width], ACT.Silu, bias=vecs[:, 8 + j : 9 + j])
                 nc.sync.dma_start(out_rows[:, 2 * jp : 2 * jp + 2, m0 : m0 + width], y_sb[:])
-            m0 = m0 + width
+
+        pick(0)
+        for n, (c, t) in enumerate(steps):
+            if n + 1 < len(steps):
+                pick(n + 1)
+            combine(n)
+            if n == 0:
+                nc.vector.quantize_mx(
+                    out=we_codes[:].bitcast(FP8X4), scales=we_sc[:], in_=we_bf[:].rearrange("p n t -> p (n t)")
+                )
+            if t == 1 and c > 0:
+                finish(c - 1)
+            if t == SLOTS - 1:
+                weave(c)
+        finish(len(CHUNKS) - 1)

@@ -22,7 +22,7 @@ PASSES = 2
 SLOTS = 4
 BANK = 512
 HALVES = S // BANK
-CHUNKS = (256, 128, 128)
+CHUNKS = (256, 256)
 
 
 def tile_list_dispense_stroke_correction_kernel(
@@ -48,10 +48,10 @@ def tile_list_dispense_stroke_correction_kernel(
 
         nc.sync.dma_start(pos1_sb[:], pos1)
         nc.sync.dma_start(pos2_sb[:], pos2)
-        scale_win = stage.tile([P, T // 4], I32, name="scale_win", offset=7168)
+        scale_win = sb([P, T // 4], I32, "scale_win")
         nc.vector.memset(scale_win[:], 0)
         nc.sync.dma_start(scale_win[0:P:4, :], tab_scales.rearrange("a q c -> q a c").bitcast(I32))
-        wd_raw = sb([P, PASSES, H // 2], I32, "wd_raw")
+        wd_raw = stage.tile([P, PASSES, H // 2], I32, name="wd_raw", offset=7168)
         nc.sync.dma_start(wd_raw[:], wd_words.rearrange("a p c -> p a c").bitcast(I32))
         wds_raw = sb([P, PASSES, H // 4], I32, "wds_raw")
         nc.gpsimd.memset(wds_raw[:], 0)
@@ -83,15 +83,11 @@ def tile_list_dispense_stroke_correction_kernel(
         picked_scales = sb([P, S], U8, "picked_scales")
         nc.vector.tensor_copy(picked_scales[:], scale_win[:].bitcast(U8).indirect(offs_sb[:]))
         picked_i32 = picked_scales[:].bitcast(I32)
-        wa_raw = []
         for a in range(PASSES):
             for d in range(4):
-                nc.sync.dma_start(
+                nc.scalar.dma_start(
                     plane_tiles[a][32 * d : 32 * d + 4, :], picked_i32[32 * d + 4 * a : 32 * d + 32 : 8, :]
                 )
-            raw = stage.tile([P, SLOTS, H], F32, name="wa_raw%d" % a, offset=8192 * a)
-            nc.sync.dma_start(raw[:], wa[512 * a : 512 * (a + 1), :].rearrange("(p j) c -> p j c", j=4))
-            wa_raw.append(raw)
         planes = [plane[:].bitcast(U8) for plane in plane_tiles]
 
         wd_sb = sb([P, PASSES * H // 2], I32, "wd_sb")
@@ -104,6 +100,11 @@ def tile_list_dispense_stroke_correction_kernel(
             wds_sb[:].rearrange("p (a t b w) -> p a t b w", a=PASSES, t=4, w=2),
             wds_raw[:].rearrange("p a (b t w) -> p a t b w", t=4, w=2),
         )
+        wa_raw = []
+        for a in range(PASSES):
+            raw = stage.tile([P, SLOTS, H], F32, name="wa_raw%d" % a, offset=8192 * a)
+            nc.sync.dma_start(raw[:], wa[512 * a : 512 * (a + 1), :].rearrange("(p j) c -> p j c", j=4))
+            wa_raw.append(raw)
         picked = []
         for a in range(PASSES):
             row = []
@@ -166,16 +167,10 @@ def tile_list_dispense_stroke_correction_kernel(
 
         b_pick = []
         for t in range(SLOTS):
-            if t < 2:
-                b_sb = sb([P, S], F32, "b_sb%d" % t)
-            else:
-                b_sb = stage.tile([P, S], F32, name="b_sb%d" % t, offset=10240 + 4096 * (t - 2))
+            b_sb = sb([P, S], F32, "b_sb%d" % t)
             for h in range(HALVES):
                 nc.scalar.copy(b_sb[:, BANK * h : BANK * (h + 1)], b_ps[(t, h)][:])
-            if t == 1:
-                g2 = stage.tile([P, M], F32, name="b_pick%d" % t, offset=8192)
-            else:
-                g2 = sb([P, M], F32, "b_pick%d" % t)
+            g2 = stage.tile([P, M], F32, name="b_pick%d" % t, offset=8192 + 2048 * t)
             nc.vector.tensor_copy(g2[:], b_sb[:].indirect(pos2_sb[:]))
             b_pick.append(g2)
 
@@ -183,10 +178,13 @@ def tile_list_dispense_stroke_correction_kernel(
         nc.tensor.transpose(vec_ps[:, 0:P], vec_rows[:], ident[:])
         vecs = sb([P, 16], F32, "vecs")
         nc.scalar.copy(vecs[:], vec_ps[:, 0:16])
+        last_bias = stage.tile([P, 16], F32, name="last_bias", offset=16384 + 1024 - 32)
+        nc.scalar.copy(last_bias[:, 0:1], vec_ps[:, SLOTS - 1 : SLOTS])
 
         a_sb = []
         for t in range(SLOTS):
             th = sb([P, S], F32, "a_sb%d" % t)
+            bias = last_bias[:, 0:1] if t == SLOTS - 1 else vecs[:, t : t + 1]
             for h in range(HALVES):
                 ps = bank(SLOTS * h + t)
                 for a in range(PASSES):
@@ -199,7 +197,7 @@ def tile_list_dispense_stroke_correction_kernel(
                         start=(a == 0),
                         stop=(a == PASSES - 1),
                     )
-                nc.scalar.activation(th[:, BANK * h : BANK * (h + 1)], ps[:], ACT.Tanh, bias=vecs[:, t : t + 1])
+                nc.scalar.activation(th[:, BANK * h : BANK * (h + 1)], ps[:], ACT.Tanh, bias=bias)
             a_sb.append(th)
 
         we_bf = sb([P, N, SLOTS], BF16, "we_bf")
@@ -214,35 +212,36 @@ def tile_list_dispense_stroke_correction_kernel(
 
         out_rows = out.rearrange("(j p) m -> p j m", p=P)
         starts = [sum(CHUNKS[:c]) for c in range(len(CHUNKS))]
-        steps = [(c, t) for c in range(len(CHUNKS)) for t in range(SLOTS)]
         z_rows = [sb([P, SLOTS, width], BF16, "z_rows%d" % c) for c, width in enumerate(CHUNKS)]
-        a_pick = {}
 
-        def pick(n):
-            c, t = steps[n]
-            m0, width = starts[c], CHUNKS[c]
-            tag = "z_bf%d" % (c - 1) if c > 0 and t == SLOTS - 1 else "a_pick%d" % (n % 3)
-            a_pick[n] = sb([P, width], F32, "a_pick%d" % n, tag)
-            nc.vector.tensor_copy(a_pick[n][:], a_sb[t][:].indirect(pos1_sb[:, m0 // 16 : (m0 + width) // 16]))
+        def pick_and_combine(steps):
+            a_pick = []
+            for t, c in steps:
+                if t == 2:
+                    g1 = stage.tile([P, CHUNKS[c]], F32, name="a_pick%d%d" % (t, c), offset=16384 + 1024 * c)
+                else:
+                    g1 = sb([P, CHUNKS[c]], F32, "a_pick%d%d" % (t, c))
+                cols = pos1_sb[:, starts[c] // 16 : (starts[c] + CHUNKS[c]) // 16]
+                nc.vector.tensor_copy(g1[:], a_sb[t][:].indirect(cols))
+                a_pick.append(g1)
+            for g1, (t, c) in zip(a_pick, steps):
+                nc.vector.scalar_tensor_tensor(
+                    z_rows[c][:, t, :], g1[:], vecs[:, 4 + t : 5 + t],
+                    b_pick[t][:, starts[c] : starts[c] + CHUNKS[c]], ALU.mult, ALU.subtract,
+                )
 
-        def combine(n):
-            c, t = steps[n]
-            m0, width = starts[c], CHUNKS[c]
-            nc.vector.scalar_tensor_tensor(
-                z_rows[c][:, t, :], a_pick[n][:], vecs[:, 4 + t : 5 + t], b_pick[t][:, m0 : m0 + width],
-                ALU.mult, ALU.subtract,
-            )
+        pick_and_combine([(0, 0), (0, 1)])
+        nc.vector.quantize_mx(
+            out=we_codes[:].bitcast(FP8X4), scales=we_sc[:], in_=we_bf[:].rearrange("p n t -> p (n t)")
+        )
+        pick_and_combine([(1, 0), (1, 1)])
+        pick_and_combine([(2, 0), (3, 0)])
+        pick_and_combine([(2, 1), (3, 1)])
 
-        z_bf = {}
-
-        def weave(c):
-            z_bf[c] = sb([P, CHUNKS[c], SLOTS], BF16, "z_bf%d" % c)
-            if c < len(CHUNKS) - 1:
-                nc.scalar.copy(z_bf[c][:], z_rows[c][:].rearrange("p t m -> p m t"))
-            else:
-                nc.vector.tensor_copy(z_bf[c][:], z_rows[c][:].rearrange("p t m -> p m t"))
-
-        def finish(c):
+        z_bf = [sb([P, width, SLOTS], BF16, "z_bf%d" % c) for c, width in enumerate(CHUNKS)]
+        nc.scalar.copy(z_bf[0][:], z_rows[0][:].rearrange("p t m -> p m t"))
+        nc.vector.tensor_copy(z_bf[1][:], z_rows[1][:].rearrange("p t m -> p m t"))
+        for c in (0, 1):
             m0, width = starts[c], CHUNKS[c]
             z_codes = sb([P, width], U32, "z_codes%d" % c)
             z_sc = sb([P, width], U8, "z_sc%d" % c)
@@ -265,18 +264,3 @@ def tile_list_dispense_stroke_correction_kernel(
                     )
                     nc.scalar.activation(y_sb[:, jj, :], ps[:, 0:width], ACT.Silu, bias=vecs[:, 8 + j : 9 + j])
                 nc.sync.dma_start(out_rows[:, 2 * jp : 2 * jp + 2, m0 : m0 + width], y_sb[:])
-
-        pick(0)
-        for n, (c, t) in enumerate(steps):
-            if n + 1 < len(steps):
-                pick(n + 1)
-            combine(n)
-            if n == 0:
-                nc.vector.quantize_mx(
-                    out=we_codes[:].bitcast(FP8X4), scales=we_sc[:], in_=we_bf[:].rearrange("p n t -> p (n t)")
-                )
-            if t == 1 and c > 0:
-                finish(c - 1)
-            if t == SLOTS - 1:
-                weave(c)
-        finish(len(CHUNKS) - 1)

@@ -18,11 +18,23 @@ ACT = mybir.ActivationFunctionType
 ALU = mybir.AluOpType
 
 P = 128
-PASSES = 2
+PASSES = K // 512
 SLOTS = 4
+QUADS = 4
 BANK = 512
-HALVES = S // BANK
-CHUNKS = (256, 256)
+BANKS = 8
+S_HALVES = S // BANK
+M_HALF = M // 2
+LIST_ROWS = 16
+OUT_TILES = N // P
+
+BA_AT, GA_AT, BE_AT, VEC_ROWS = 0, SLOTS, 2 * SLOTS, 2 * SLOTS + OUT_TILES
+
+WORDS1_AT = 0
+WA0_HALF1_AT = WORDS1_AT + 4 * T
+SCALE_WIN_AT = WA0_HALF1_AT - T // 2
+PICKS2_AT = 20480
+LAST_BIAS_AT = PICKS2_AT + 4 * M_HALF - 64
 
 
 def tile_list_dispense_stroke_correction_kernel(
@@ -38,39 +50,47 @@ def tile_list_dispense_stroke_correction_kernel(
         def sb(shape, dtype, name, tag=None):
             return keep.tile(shape, dtype, name=name, tag=tag or name, align_bytes=64)
 
-        def bank(i):
-            return psum.tile([P, BANK], F32, name="bank", tag="bank%d" % (i % 8))
+        def placed(shape, dtype, name, offset):
+            return stage.tile(shape, dtype, name=name, offset=offset, align_bytes=64)
 
-        offs_sb = lists.tile([P, S // 16], U16, name="offs_sb")
-        pos1_sb = lists.tile([P, M // 16], U16, name="pos1_sb")
-        pos2_sb = lists.tile([P, M // 16], U16, name="pos2_sb")
+        def bank(number):
+            return psum.tile([P, BANK], F32, name="bank", tag="bank%d" % (number % BANKS))
+
+        offs_sb = lists.tile([P, S // LIST_ROWS], U16, name="offs_sb")
+        pos1_sb = lists.tile([P, M // LIST_ROWS], U16, name="pos1_sb")
+        pos2_sb = lists.tile([P, M // LIST_ROWS], U16, name="pos2_sb")
         nc.sync.dma_start(offs_sb[:], offs)
-
         nc.sync.dma_start(pos1_sb[:], pos1)
         nc.sync.dma_start(pos2_sb[:], pos2)
-        scale_win = sb([P, T // 4], I32, "scale_win")
+
+        scale_win = placed([P, T // 4], I32, "scale_win", SCALE_WIN_AT)
         nc.vector.memset(scale_win[:], 0)
         nc.sync.dma_start(scale_win[0:P:4, :], tab_scales.rearrange("a q c -> q a c").bitcast(I32))
-        wd_raw = stage.tile([P, PASSES, H // 2], I32, name="wd_raw", offset=7168)
+        wd_raw = sb([P, PASSES, H // 2], I32, "wd_raw")
         nc.sync.dma_start(wd_raw[:], wd_words.rearrange("a p c -> p a c").bitcast(I32))
-        wds_raw = sb([P, PASSES, H // 4], I32, "wds_raw")
-        nc.gpsimd.memset(wds_raw[:], 0)
-        word_win = []
-        for a in range(PASSES):
-            win = sb([P, T], I32, "word_win%d" % a)
-            nc.sync.dma_start(win[:], tab_words[a].rearrange("p t i -> p (t i)").bitcast(I32))
-            word_win.append(win)
-            if a == 0:
-                for d in range(4):
-                    nc.sync.dma_start(
-                        wds_raw[32 * d : 32 * d + 4, :, :],
-                        wd_scales[:, 4 * d : 4 * d + 4, :].rearrange("a r c -> r a c").bitcast(I32),
-                    )
+        wd_scale_raw = sb([P, PASSES, H // 4], I32, "wd_scale_raw")
+        nc.gpsimd.memset(wd_scale_raw[:], 0)
 
-        warm_in = sb([P, 8], F32, "warm_in")
-        warm_out = sb([P, 8], F32, "warm_out")
-        nc.vector.memset(warm_in[:], 0.0)
-        nc.scalar.activation(warm_out[:], warm_in[:], ACT.Silu)
+        word_win = [sb([P, T], I32, "word_win0"), placed([P, T], I32, "word_win1", WORDS1_AT)]
+        wa0_raw = [
+            sb([P, SLOTS, H // 2], F32, "wa0_raw0"),
+            placed([P, SLOTS, H // 2], F32, "wa0_raw1", WA0_HALF1_AT),
+        ]
+        wa_rows = wa.rearrange("(a p i) r -> a p i r", a=PASSES, i=SLOTS)
+
+        def load_words(a):
+            nc.sync.dma_start(word_win[a][:], tab_words[a].rearrange("p t i -> p (t i)").bitcast(I32))
+
+        def load_wa0(half):
+            nc.sync.dma_start(wa0_raw[half][:], wa_rows[0][:, :, H // 2 * half : H // 2 * (half + 1)])
+
+        load_words(0)
+        for d in range(QUADS):
+            nc.sync.dma_start(
+                wd_scale_raw[32 * d : 32 * d + 4, :, :],
+                wd_scales[:, 4 * d : 4 * d + 4, :].rearrange("a s c -> s a c").bitcast(I32),
+            )
+        load_wa0(0)
 
         plane_tiles = []
         for a in range(PASSES):
@@ -82,185 +102,199 @@ def tile_list_dispense_stroke_correction_kernel(
 
         picked_scales = sb([P, S], U8, "picked_scales")
         nc.vector.tensor_copy(picked_scales[:], scale_win[:].bitcast(U8).indirect(offs_sb[:]))
-        picked_i32 = picked_scales[:].bitcast(I32)
+        picked_scales_i32 = picked_scales[:].bitcast(I32)
         for a in range(PASSES):
-            for d in range(4):
-                nc.scalar.dma_start(
-                    plane_tiles[a][32 * d : 32 * d + 4, :], picked_i32[32 * d + 4 * a : 32 * d + 32 : 8, :]
+            for d in range(QUADS):
+                nc.sync.dma_start(
+                    plane_tiles[a][32 * d : 32 * d + 4, :],
+                    picked_scales_i32[32 * d + 4 * a : 32 * d + 32 : 8, :],
                 )
+            if a == 0:
+                load_words(1)
+                load_wa0(1)
         planes = [plane[:].bitcast(U8) for plane in plane_tiles]
 
         wd_sb = sb([P, PASSES * H // 2], I32, "wd_sb")
         nc.vector.tensor_copy(
-            wd_sb[:].rearrange("p (a t b w) -> p a t b w", a=PASSES, t=4, w=4),
-            wd_raw[:].rearrange("p a (b t w) -> p a t b w", t=4, w=4),
+            wd_sb[:].rearrange("p (a t b w) -> p a t b w", a=PASSES, t=SLOTS, w=4),
+            wd_raw[:].rearrange("p a (b t w) -> p a t b w", t=SLOTS, w=4),
         )
-        wds_sb = sb([P, PASSES * H // 4], I32, "wds_sb")
+        wd_scale_sb = sb([P, PASSES * H // 4], I32, "wd_scale_sb")
         nc.vector.tensor_copy(
-            wds_sb[:].rearrange("p (a t b w) -> p a t b w", a=PASSES, t=4, w=2),
-            wds_raw[:].rearrange("p a (b t w) -> p a t b w", t=4, w=2),
+            wd_scale_sb[:].rearrange("p (a t b w) -> p a t b w", a=PASSES, t=SLOTS, w=2),
+            wd_scale_raw[:].rearrange("p a (b t w) -> p a t b w", t=SLOTS, w=2),
         )
-        wa_raw = []
-        for a in range(PASSES):
-            raw = stage.tile([P, SLOTS, H], F32, name="wa_raw%d" % a, offset=8192 * a)
-            nc.sync.dma_start(raw[:], wa[512 * a : 512 * (a + 1), :].rearrange("(p j) c -> p j c", j=4))
-            wa_raw.append(raw)
-        picked = []
-        for a in range(PASSES):
-            row = []
-            for h in range(HALVES):
-                g = sb([P, BANK], U32, "picked%d%d" % (a, h))
-                nc.vector.tensor_copy(g[:], word_win[a][:].bitcast(U32).indirect(offs_sb[:, 32 * h : 32 * (h + 1)]))
-                row.append(g)
-            picked.append(row)
 
+        half_cols = BANK // LIST_ROWS
+        picked_words = {}
+        for a in range(PASSES):
+            for h in range(S_HALVES):
+                picked_words[(a, h)] = sb([P, BANK], U32, "picked_words%d%d" % (a, h))
+                nc.vector.tensor_copy(
+                    picked_words[(a, h)][:],
+                    word_win[a][:].bitcast(U32).indirect(offs_sb[:, half_cols * h : half_cols * (h + 1)]),
+                )
+            if a == 0:
+                wa1_raw = sb([P, SLOTS, H], F32, "wa1_raw", "word_win0")
+                nc.sync.dma_start(wa1_raw[:], wa_rows[1])
 
-        vec_rows = sb([P, P], F32, "vec_rows", "wds_raw")
-        nc.gpsimd.memset(vec_rows[:], 0.0)
-        for row0, vec in ((0, ba), (4, ga)):
-            nc.sync.dma_start(
-                vec_rows[row0 : row0 + 4, :].rearrange("t (b i) -> t b i", i=8),
-                vec.rearrange("(b t i) -> t b i", t=4, i=8),
+        def table_pass(acc, lhsT, lhsT_scale, a, h):
+            nc.tensor.matmul_mx(
+                out=acc[:],
+                lhsT=lhsT,
+                lhsT_scale=lhsT_scale,
+                rhs=picked_words[(a, h)][:].bitcast(FP8X4),
+                rhs_scale=planes[a][:, BANK * h : BANK * (h + 1)],
+                start=(a == 0),
+                stop=(a == PASSES - 1),
             )
-        nc.sync.dma_start(vec_rows[8:12, :], be.rearrange("(j p) -> j p", p=P))
 
         wd_u8 = wd_sb[:].bitcast(U8)
-        wds_u8 = wds_sb[:].bitcast(U8)
+        wd_scale_u8 = wd_scale_sb[:].bitcast(U8)
         b_ps = {}
         for t in range(SLOTS):
             for a in range(PASSES):
-                for h in range(HALVES):
+                for h in range(S_HALVES):
                     if a == 0:
                         b_ps[(t, h)] = bank(SLOTS * h + t)
-                    c0 = a * H + t * P
-                    nc.tensor.matmul_mx(
-                        out=b_ps[(t, h)][:],
-                        lhsT=wd_u8[:, 2 * c0 : 2 * (c0 + P)].bitcast(FP4X4),
-                        lhsT_scale=wds_u8[:, c0 : c0 + P],
-                        rhs=picked[a][h][:].bitcast(FP8X4),
-                        rhs_scale=planes[a][:, BANK * h : BANK * (h + 1)],
-                        start=(a == 0),
-                        stop=(a == PASSES - 1),
+                    col = a * H + t * P
+                    table_pass(
+                        b_ps[(t, h)],
+                        wd_u8[:, 2 * col : 2 * (col + P)].bitcast(FP4X4),
+                        wd_scale_u8[:, col : col + P],
+                        a,
+                        h,
                     )
 
-        wa_codes, wa_sc = [], []
-        for a in range(PASSES):
-            wa_bf = sb([P, SLOTS * H], BF16, "wa_bf%d" % a)
-            dst = wa_bf[:].rearrange("p (t b i j) -> p t b i j", t=4, i=8, j=4)
-            src = wa_raw[a][:].rearrange("p j (b t i) -> p t b i j", t=4, i=8)
-            if a == 0:
-                nc.scalar.copy(dst[:, 0:2], src[:, 0:2])
-            else:
-                nc.scalar.copy(dst[:, 0], src[:, 0])
-                nc.vector.tensor_copy(dst[:, 1], src[:, 1])
-            nc.vector.tensor_copy(dst[:, 2:4], src[:, 2:4])
-            codes = sb([P, H], U32, "wa_codes%d" % a)
-            sc = sb([P, H], U8, "wa_sc%d" % a)
-            nc.vector.quantize_mx(out=codes[:].bitcast(FP8X4), scales=sc[:], in_=wa_bf[:])
-            wa_codes.append(codes)
-            wa_sc.append(sc)
+        wa_codes = [sb([P, H], U32, "wa_codes%d" % a) for a in range(PASSES)]
+        wa_scales = [sb([P, H], U8, "wa_scales%d" % a) for a in range(PASSES)]
+        wa0_bf = sb([P, SLOTS * H], BF16, "wa0_bf")
+        wa0_dealt = wa0_bf[:].rearrange("p (t b i e) -> p t b i e", t=SLOTS, i=8, e=4)
+        for half in range(2):
+            nc.scalar.copy(
+                wa0_dealt[:, :, 8 * half : 8 * (half + 1)],
+                wa0_raw[half][:].rearrange("p e (b t i) -> p t b i e", t=SLOTS, i=8),
+            )
+        nc.vector.quantize_mx(out=wa_codes[0][:].bitcast(FP8X4), scales=wa_scales[0][:], in_=wa0_bf[:])
+        wa1_by_slot = wa1_raw[:].rearrange("p e (b t i) -> p t b i e", t=SLOTS, i=8)
+        for pair in range(SLOTS // 2):
+            wa1_bf = sb([P, 2 * H], BF16, "wa1_bf%d" % pair)
+            wa1_dealt = wa1_bf[:].rearrange("p (t b i e) -> p t b i e", t=2, i=8, e=4)
+            for u in range(2):
+                nc.gpsimd.tensor_scalar(wa1_dealt[:, u], wa1_by_slot[:, 2 * pair + u], 1.0, 0.0, ALU.mult, ALU.add)
+            cols = slice(2 * P * pair, 2 * P * (pair + 1))
+            nc.vector.quantize_mx(
+                out=wa_codes[1][:, cols].bitcast(FP8X4), scales=wa_scales[1][:, cols], in_=wa1_bf[:]
+            )
 
-        we_raw = stage.tile([P, SLOTS, N], F32, name="we_raw", offset=0)
-        we_rows = we.rearrange("(b t i) n -> t b i n", t=4, i=8)
+        vec_rows = sb([P, P], F32, "vec_rows", "wa0_raw0")
+        nc.gpsimd.memset(vec_rows[:], 0.0)
+        for row, vec in ((BA_AT, ba), (GA_AT, ga)):
+            nc.sync.dma_start(
+                vec_rows[row : row + SLOTS, :].rearrange("t (b i) -> t b i", i=8),
+                vec.rearrange("(b t i) -> t b i", t=SLOTS, i=8),
+            )
+        nc.sync.dma_start(vec_rows[BE_AT:VEC_ROWS, :], be.rearrange("(j p) -> j p", p=P))
+
+        we_raw = placed([P, SLOTS, N], F32, "we_raw", WORDS1_AT)
+        we_rows = we.rearrange("(b t i) n -> t b i n", t=SLOTS, i=8)
         for t in range(SLOTS):
             nc.sync.dma_start(we_raw[:, t, :], we_rows[t])
 
         b_pick = []
         for t in range(SLOTS):
             b_sb = sb([P, S], F32, "b_sb%d" % t)
-            for h in range(HALVES):
-                nc.scalar.copy(b_sb[:, BANK * h : BANK * (h + 1)], b_ps[(t, h)][:])
-            g2 = stage.tile([P, M], F32, name="b_pick%d" % t, offset=8192 + 2048 * t)
-            nc.vector.tensor_copy(g2[:], b_sb[:].indirect(pos2_sb[:]))
-            b_pick.append(g2)
+            for h in range(S_HALVES):
+                empty_bank = nc.vector.tensor_copy if (t, h) == (0, 1) else nc.scalar.copy
+                empty_bank(b_sb[:, BANK * h : BANK * (h + 1)], b_ps[(t, h)][:])
+            pick = sb([P, M], F32, "b_pick%d" % t, "wa1_bf%d" % (t - 2) if t >= 2 else None)
+            nc.vector.tensor_copy(pick[:], b_sb[:].indirect(pos2_sb[:]))
+            b_pick.append(pick)
 
         vec_ps = bank(1)
         nc.tensor.transpose(vec_ps[:, 0:P], vec_rows[:], ident[:])
-        vecs = sb([P, 16], F32, "vecs")
-        nc.scalar.copy(vecs[:], vec_ps[:, 0:16])
-        last_bias = stage.tile([P, 16], F32, name="last_bias", offset=16384 + 1024 - 32)
-        nc.scalar.copy(last_bias[:, 0:1], vec_ps[:, SLOTS - 1 : SLOTS])
+        vecs = sb([P, VEC_ROWS], F32, "vecs")
+        nc.scalar.copy(vecs[:], vec_ps[:, 0:VEC_ROWS])
+        last = SLOTS - 1
+        last_bias = placed([P, 32], F32, "last_bias", LAST_BIAS_AT)
+        nc.scalar.copy(last_bias[:, 0:1], vec_ps[:, BA_AT + last : BA_AT + last + 1])
 
-        a_sb = []
+        tanh_sb = []
         for t in range(SLOTS):
-            th = sb([P, S], F32, "a_sb%d" % t)
-            bias = last_bias[:, 0:1] if t == SLOTS - 1 else vecs[:, t : t + 1]
-            for h in range(HALVES):
-                ps = bank(SLOTS * h + t)
+            rows = sb([P, S], F32, "tanh_sb%d" % t)
+            bias = last_bias[:, 0:1] if t == last else vecs[:, BA_AT + t : BA_AT + t + 1]
+            for h in range(S_HALVES):
+                acc = bank(SLOTS * h + t)
                 for a in range(PASSES):
-                    nc.tensor.matmul_mx(
-                        out=ps[:],
-                        lhsT=wa_codes[a][:, t * P : (t + 1) * P].bitcast(FP8X4),
-                        lhsT_scale=wa_sc[a][:, t * P : (t + 1) * P],
-                        rhs=picked[a][h][:].bitcast(FP8X4),
-                        rhs_scale=planes[a][:, BANK * h : BANK * (h + 1)],
-                        start=(a == 0),
-                        stop=(a == PASSES - 1),
+                    table_pass(
+                        acc,
+                        wa_codes[a][:, t * P : (t + 1) * P].bitcast(FP8X4),
+                        wa_scales[a][:, t * P : (t + 1) * P],
+                        a,
+                        h,
                     )
-                nc.scalar.activation(th[:, BANK * h : BANK * (h + 1)], ps[:], ACT.Tanh, bias=bias)
-            a_sb.append(th)
+                nc.scalar.activation(rows[:, BANK * h : BANK * (h + 1)], acc[:], ACT.Tanh, bias=bias)
+            tanh_sb.append(rows)
 
-        we_bf = sb([P, N, SLOTS], BF16, "we_bf")
-        for j in range(4):
-            nc.gpsimd.tensor_scalar(
-                we_bf[:, j * P : (j + 1) * P, :],
-                we_raw[:, :, j * P : (j + 1) * P].rearrange("p t n -> p n t"),
-                1.0, 0.0, ALU.mult, ALU.add,
-            )
+        we_bf = sb([P, N, SLOTS], BF16, "we_bf", "wa_codes1")
+        nc.scalar.copy(we_bf[:], we_raw[:].rearrange("p t n -> p n t"))
         we_codes = sb([P, N], U32, "we_codes")
-        we_sc = sb([P, N], U8, "we_sc")
+        we_scales = sb([P, N], U8, "we_scales")
 
-        out_rows = out.rearrange("(j p) m -> p j m", p=P)
-        starts = [sum(CHUNKS[:c]) for c in range(len(CHUNKS))]
-        z_rows = [sb([P, SLOTS, width], BF16, "z_rows%d" % c) for c, width in enumerate(CHUNKS)]
+        z_rows = [sb([P, SLOTS, M_HALF], BF16, "z_rows%d" % c) for c in range(2)]
+        pos_cols = M_HALF // LIST_ROWS
 
-        def pick_and_combine(steps):
-            a_pick = []
+        def pick_and_subtract(steps):
+            tanh_pick = []
             for t, c in steps:
+                name = "tanh_pick%d%d" % (t, c)
                 if t == 2:
-                    g1 = stage.tile([P, CHUNKS[c]], F32, name="a_pick%d%d" % (t, c), offset=16384 + 1024 * c)
+                    pick = placed([P, M_HALF], F32, name, PICKS2_AT + 4 * M_HALF * c)
                 else:
-                    g1 = sb([P, CHUNKS[c]], F32, "a_pick%d%d" % (t, c))
-                cols = pos1_sb[:, starts[c] // 16 : (starts[c] + CHUNKS[c]) // 16]
-                nc.vector.tensor_copy(g1[:], a_sb[t][:].indirect(cols))
-                a_pick.append(g1)
-            for g1, (t, c) in zip(a_pick, steps):
+                    pick = sb([P, M_HALF], F32, name)
+                nc.vector.tensor_copy(pick[:], tanh_sb[t][:].indirect(pos1_sb[:, pos_cols * c : pos_cols * (c + 1)]))
+                tanh_pick.append(pick)
+            for pick, (t, c) in zip(tanh_pick, steps):
                 nc.vector.scalar_tensor_tensor(
-                    z_rows[c][:, t, :], g1[:], vecs[:, 4 + t : 5 + t],
-                    b_pick[t][:, starts[c] : starts[c] + CHUNKS[c]], ALU.mult, ALU.subtract,
+                    z_rows[c][:, t, :],
+                    pick[:],
+                    vecs[:, GA_AT + t : GA_AT + t + 1],
+                    b_pick[t][:, M_HALF * c : M_HALF * (c + 1)],
+                    ALU.mult,
+                    ALU.subtract,
                 )
 
-        pick_and_combine([(0, 0), (0, 1)])
+        pick_and_subtract([(0, 0), (0, 1)])
+        pick_and_subtract([(1, 0), (1, 1)])
+        pick_and_subtract([(2, 0), (3, 0)])
         nc.vector.quantize_mx(
-            out=we_codes[:].bitcast(FP8X4), scales=we_sc[:], in_=we_bf[:].rearrange("p n t -> p (n t)")
+            out=we_codes[:].bitcast(FP8X4), scales=we_scales[:], in_=we_bf[:].rearrange("p n t -> p (n t)")
         )
-        pick_and_combine([(1, 0), (1, 1)])
-        pick_and_combine([(2, 0), (3, 0)])
-        pick_and_combine([(2, 1), (3, 1)])
+        pick_and_subtract([(2, 1), (3, 1)])
 
-        z_bf = [sb([P, width, SLOTS], BF16, "z_bf%d" % c) for c, width in enumerate(CHUNKS)]
-        nc.scalar.copy(z_bf[0][:], z_rows[0][:].rearrange("p t m -> p m t"))
-        nc.vector.tensor_copy(z_bf[1][:], z_rows[1][:].rearrange("p t m -> p m t"))
-        for c in (0, 1):
-            m0, width = starts[c], CHUNKS[c]
-            z_codes = sb([P, width], U32, "z_codes%d" % c)
-            z_sc = sb([P, width], U8, "z_sc%d" % c)
+        out_rows = out.rearrange("(j p) m -> p j m", p=P)
+        for c, interleave in enumerate((nc.scalar.copy, nc.vector.tensor_copy)):
+            z_bf = sb([P, M_HALF, SLOTS], BF16, "z_bf%d" % c, "z_bf")
+            interleave(z_bf[:], z_rows[c][:].rearrange("p t m -> p m t"))
+            z_codes = sb([P, M_HALF], U32, "z_codes%d" % c)
+            z_scales = sb([P, M_HALF], U8, "z_scales%d" % c)
             nc.vector.quantize_mx(
-                out=z_codes[:].bitcast(FP8X4), scales=z_sc[:], in_=z_bf[c][:].rearrange("p m t -> p (m t)")
+                out=z_codes[:].bitcast(FP8X4), scales=z_scales[:], in_=z_bf[:].rearrange("p m t -> p (m t)")
             )
-            for jp in range(2):
-                y_sb = sb([P, 2, width], F32, "y_sb%d%d" % (c, jp))
-                for jj in range(2):
-                    j = 2 * jp + jj
-                    ps = bank(4 * c + j)
+            for j0 in range(0, OUT_TILES, 2):
+                y_sb = sb([P, 2, M_HALF], F32, "y_sb%d%d" % (c, j0))
+                for j in (j0, j0 + 1):
+                    acc = bank(OUT_TILES * c + j)
                     nc.tensor.matmul_mx(
-                        out=ps[:, 0:width],
+                        out=acc[:, 0:M_HALF],
                         lhsT=we_codes[:, j * P : (j + 1) * P].bitcast(FP8X4),
-                        lhsT_scale=we_sc[:, j * P : (j + 1) * P],
+                        lhsT_scale=we_scales[:, j * P : (j + 1) * P],
                         rhs=z_codes[:].bitcast(FP8X4),
-                        rhs_scale=z_sc[:],
+                        rhs_scale=z_scales[:],
                         start=True,
                         stop=True,
                     )
-                    nc.scalar.activation(y_sb[:, jj, :], ps[:, 0:width], ACT.Silu, bias=vecs[:, 8 + j : 9 + j])
-                nc.sync.dma_start(out_rows[:, 2 * jp : 2 * jp + 2, m0 : m0 + width], y_sb[:])
+                    nc.scalar.activation(
+                        y_sb[:, j - j0, :], acc[:, 0:M_HALF], ACT.Silu, bias=vecs[:, BE_AT + j : BE_AT + j + 1]
+                    )
+                nc.sync.dma_start(out_rows[:, j0 : j0 + 2, M_HALF * c : M_HALF * (c + 1)], y_sb[:])

from contextlib import ExitStack

import concourse.mybir as mybir
from concourse.masks import make_identity

K, T, S, M, H, N = 1024, 2048, 1024, 512, 512, 512
FLOPS = 2 * (2 * K * H * S + H * N * M)

F32 = mybir.dt.float32
BF16 = mybir.dt.bfloat16
I32 = mybir.dt.int32
U32 = mybir.dt.uint32
U16 = mybir.dt.uint16
U8 = mybir.dt.uint8
FP8X4 = mybir.dt.float8_e4m3fn_x4
FP4X4 = mybir.dt.float4_e2m1fn_x4
ACT = mybir.ActivationFunctionType
ALU = mybir.AluOpType

P = 128
PASSES = K // 512
SLOTS = 4
QUADS = 4
BANK = 512
BANKS = 8
S_HALVES = S // BANK
M_HALF = M // 2
LIST_ROWS = 16
OUT_TILES = N // P

BA_AT, GA_AT, BE_AT, VEC_ROWS = 0, SLOTS, 2 * SLOTS, 2 * SLOTS + OUT_TILES

WORDS1_AT = 0
WA0_HALF1_AT = WORDS1_AT + 4 * T
SCALE_WIN_AT = WA0_HALF1_AT - T // 2
PICKS2_AT = 20480
LAST_BIAS_AT = PICKS2_AT + 4 * M_HALF - 64


def tile_list_dispense_stroke_correction_kernel(
    tc, tab_words, tab_scales, offs, wa, ba, ga, wd_words, wd_scales, pos1, pos2, we, be, out
):
    nc = tc.nc
    with ExitStack() as ctx:
        lists = ctx.enter_context(tc.tile_pool(name="lists", bufs=1))
        keep = ctx.enter_context(tc.tile_pool(name="keep", bufs=1))
        stage = ctx.enter_context(tc.tile_pool(name="stage", bufs=1))
        psum = ctx.enter_context(tc.psum_pool(name="psum", bufs=1))

        def sb(shape, dtype, name, tag=None):
            return keep.tile(shape, dtype, name=name, tag=tag or name, align_bytes=64)

        def placed(shape, dtype, name, offset):
            return stage.tile(shape, dtype, name=name, offset=offset, align_bytes=64)

        def bank(number):
            return psum.tile([P, BANK], F32, name="bank", tag="bank%d" % (number % BANKS))

        offs_sb = lists.tile([P, S // LIST_ROWS], U16, name="offs_sb")
        pos1_sb = lists.tile([P, M // LIST_ROWS], U16, name="pos1_sb")
        pos2_sb = lists.tile([P, M // LIST_ROWS], U16, name="pos2_sb")
        nc.sync.dma_start(offs_sb[:], offs)
        nc.sync.dma_start(pos1_sb[:], pos1)
        nc.sync.dma_start(pos2_sb[:], pos2)

        scale_win = placed([P, T // 4], I32, "scale_win", SCALE_WIN_AT)
        nc.vector.memset(scale_win[:], 0)
        nc.sync.dma_start(scale_win[0:P:4, :], tab_scales.rearrange("a q c -> q a c").bitcast(I32))
        wd_raw = sb([P, PASSES, H // 2], I32, "wd_raw")
        nc.sync.dma_start(wd_raw[:], wd_words.rearrange("a p c -> p a c").bitcast(I32))
        wd_scale_raw = sb([P, PASSES, H // 4], I32, "wd_scale_raw")
        nc.gpsimd.memset(wd_scale_raw[:], 0)

        word_win = [sb([P, T], I32, "word_win0"), placed([P, T], I32, "word_win1", WORDS1_AT)]
        wa0_raw = [
            sb([P, SLOTS, H // 2], F32, "wa0_raw0"),
            placed([P, SLOTS, H // 2], F32, "wa0_raw1", WA0_HALF1_AT),
        ]
        wa_rows = wa.rearrange("(a p i) r -> a p i r", a=PASSES, i=SLOTS)

        def load_words(a):
            nc.sync.dma_start(word_win[a][:], tab_words[a].rearrange("p t i -> p (t i)").bitcast(I32))

        def load_wa0(half):
            nc.sync.dma_start(wa0_raw[half][:], wa_rows[0][:, :, H // 2 * half : H // 2 * (half + 1)])

        load_words(0)
        for d in range(QUADS):
            nc.sync.dma_start(
                wd_scale_raw[32 * d : 32 * d + 4, :, :],
                wd_scales[:, 4 * d : 4 * d + 4, :].rearrange("a s c -> s a c").bitcast(I32),
            )
        load_wa0(0)

        plane_tiles = []
        for a in range(PASSES):
            plane = sb([P, S // 4], I32, "plane%d" % a)
            nc.gpsimd.memset(plane[:], 0)
            plane_tiles.append(plane)
        ident = sb([P, P], F32, "ident")
        make_identity(nc, ident[:])

        picked_scales = sb([P, S], U8, "picked_scales")
        nc.vector.tensor_copy(picked_scales[:], scale_win[:].bitcast(U8).indirect(offs_sb[:]))
        picked_scales_i32 = picked_scales[:].bitcast(I32)
        for a in range(PASSES):
            for d in range(QUADS):
                nc.sync.dma_start(
                    plane_tiles[a][32 * d : 32 * d + 4, :],
                    picked_scales_i32[32 * d + 4 * a : 32 * d + 32 : 8, :],
                )
            if a == 0:
                load_words(1)
                load_wa0(1)
        planes = [plane[:].bitcast(U8) for plane in plane_tiles]

        wd_sb = sb([P, PASSES * H // 2], I32, "wd_sb")
        nc.vector.tensor_copy(
            wd_sb[:].rearrange("p (a t b w) -> p a t b w", a=PASSES, t=SLOTS, w=4),
            wd_raw[:].rearrange("p a (b t w) -> p a t b w", t=SLOTS, w=4),
        )
        wd_scale_sb = sb([P, PASSES * H // 4], I32, "wd_scale_sb")
        nc.vector.tensor_copy(
            wd_scale_sb[:].rearrange("p (a t b w) -> p a t b w", a=PASSES, t=SLOTS, w=2),
            wd_scale_raw[:].rearrange("p a (b t w) -> p a t b w", t=SLOTS, w=2),
        )

        half_cols = BANK // LIST_ROWS
        picked_words = {}
        for a in range(PASSES):
            for h in range(S_HALVES):
                picked_words[(a, h)] = sb([P, BANK], U32, "picked_words%d%d" % (a, h))
                nc.vector.tensor_copy(
                    picked_words[(a, h)][:],
                    word_win[a][:].bitcast(U32).indirect(offs_sb[:, half_cols * h : half_cols * (h + 1)]),
                )
            if a == 0:
                wa1_raw = sb([P, SLOTS, H], F32, "wa1_raw", "word_win0")
                nc.sync.dma_start(wa1_raw[:], wa_rows[1])

        def table_pass(acc, lhsT, lhsT_scale, a, h):
            nc.tensor.matmul_mx(
                out=acc[:],
                lhsT=lhsT,
                lhsT_scale=lhsT_scale,
                rhs=picked_words[(a, h)][:].bitcast(FP8X4),
                rhs_scale=planes[a][:, BANK * h : BANK * (h + 1)],
                start=(a == 0),
                stop=(a == PASSES - 1),
            )

        wd_u8 = wd_sb[:].bitcast(U8)
        wd_scale_u8 = wd_scale_sb[:].bitcast(U8)
        b_ps = {}
        for t in range(SLOTS):
            for a in range(PASSES):
                for h in range(S_HALVES):
                    if a == 0:
                        b_ps[(t, h)] = bank(SLOTS * h + t)
                    col = a * H + t * P
                    table_pass(
                        b_ps[(t, h)],
                        wd_u8[:, 2 * col : 2 * (col + P)].bitcast(FP4X4),
                        wd_scale_u8[:, col : col + P],
                        a,
                        h,
                    )

        wa_codes = [sb([P, H], U32, "wa_codes%d" % a) for a in range(PASSES)]
        wa_scales = [sb([P, H], U8, "wa_scales%d" % a) for a in range(PASSES)]
        wa0_bf = sb([P, SLOTS * H], BF16, "wa0_bf")
        wa0_dealt = wa0_bf[:].rearrange("p (t b i e) -> p t b i e", t=SLOTS, i=8, e=4)
        for half in range(2):
            nc.scalar.copy(
                wa0_dealt[:, :, 8 * half : 8 * (half + 1)],
                wa0_raw[half][:].rearrange("p e (b t i) -> p t b i e", t=SLOTS, i=8),
            )
        nc.vector.quantize_mx(out=wa_codes[0][:].bitcast(FP8X4), scales=wa_scales[0][:], in_=wa0_bf[:])
        wa1_by_slot = wa1_raw[:].rearrange("p e (b t i) -> p t b i e", t=SLOTS, i=8)
        for pair in range(SLOTS // 2):
            wa1_bf = sb([P, 2 * H], BF16, "wa1_bf%d" % pair)
            wa1_dealt = wa1_bf[:].rearrange("p (t b i e) -> p t b i e", t=2, i=8, e=4)
            for u in range(2):
                nc.gpsimd.tensor_scalar(wa1_dealt[:, u], wa1_by_slot[:, 2 * pair + u], 1.0, 0.0, ALU.mult, ALU.add)
            cols = slice(2 * P * pair, 2 * P * (pair + 1))
            nc.vector.quantize_mx(
                out=wa_codes[1][:, cols].bitcast(FP8X4), scales=wa_scales[1][:, cols], in_=wa1_bf[:]
            )

        vec_rows = sb([P, P], F32, "vec_rows", "wa0_raw0")
        nc.gpsimd.memset(vec_rows[:], 0.0)
        for row, vec in ((BA_AT, ba), (GA_AT, ga)):
            nc.sync.dma_start(
                vec_rows[row : row + SLOTS, :].rearrange("t (b i) -> t b i", i=8),
                vec.rearrange("(b t i) -> t b i", t=SLOTS, i=8),
            )
        nc.sync.dma_start(vec_rows[BE_AT:VEC_ROWS, :], be.rearrange("(j p) -> j p", p=P))

        we_raw = placed([P, SLOTS, N], F32, "we_raw", WORDS1_AT)
        we_rows = we.rearrange("(b t i) n -> t b i n", t=SLOTS, i=8)
        for t in range(SLOTS):
            nc.sync.dma_start(we_raw[:, t, :], we_rows[t])

        b_pick = []
        for t in range(SLOTS):
            b_sb = sb([P, S], F32, "b_sb%d" % t)
            for h in range(S_HALVES):
                empty_bank = nc.vector.tensor_copy if (t, h) == (0, 1) else nc.scalar.copy
                empty_bank(b_sb[:, BANK * h : BANK * (h + 1)], b_ps[(t, h)][:])
            pick = sb([P, M], F32, "b_pick%d" % t, "wa1_bf%d" % (t - 2) if t >= 2 else None)
            nc.vector.tensor_copy(pick[:], b_sb[:].indirect(pos2_sb[:]))
            b_pick.append(pick)

        vec_ps = bank(1)
        nc.tensor.transpose(vec_ps[:, 0:P], vec_rows[:], ident[:])
        vecs = sb([P, VEC_ROWS], F32, "vecs")
        nc.scalar.copy(vecs[:], vec_ps[:, 0:VEC_ROWS])
        last = SLOTS - 1
        last_bias = placed([P, 32], F32, "last_bias", LAST_BIAS_AT)
        nc.scalar.copy(last_bias[:, 0:1], vec_ps[:, BA_AT + last : BA_AT + last + 1])

        tanh_sb = []
        for t in range(SLOTS):
            rows = sb([P, S], F32, "tanh_sb%d" % t)
            bias = last_bias[:, 0:1] if t == last else vecs[:, BA_AT + t : BA_AT + t + 1]
            for h in range(S_HALVES):
                acc = bank(SLOTS * h + t)
                for a in range(PASSES):
                    table_pass(
                        acc,
                        wa_codes[a][:, t * P : (t + 1) * P].bitcast(FP8X4),
                        wa_scales[a][:, t * P : (t + 1) * P],
                        a,
                        h,
                    )
                nc.scalar.activation(rows[:, BANK * h : BANK * (h + 1)], acc[:], ACT.Tanh, bias=bias)
            tanh_sb.append(rows)

        we_bf = sb([P, N, SLOTS], BF16, "we_bf", "wa_codes1")
        nc.scalar.copy(we_bf[:], we_raw[:].rearrange("p t n -> p n t"))
        we_codes = sb([P, N], U32, "we_codes")
        we_scales = sb([P, N], U8, "we_scales")

        z_rows = [sb([P, SLOTS, M_HALF], BF16, "z_rows%d" % c) for c in range(2)]
        pos_cols = M_HALF // LIST_ROWS

        def pick_and_subtract(steps):
            tanh_pick = []
            for t, c in steps:
                name = "tanh_pick%d%d" % (t, c)
                if t == 2:
                    pick = placed([P, M_HALF], F32, name, PICKS2_AT + 4 * M_HALF * c)
                else:
                    pick = sb([P, M_HALF], F32, name)
                nc.vector.tensor_copy(pick[:], tanh_sb[t][:].indirect(pos1_sb[:, pos_cols * c : pos_cols * (c + 1)]))
                tanh_pick.append(pick)
            for pick, (t, c) in zip(tanh_pick, steps):
                nc.vector.scalar_tensor_tensor(
                    z_rows[c][:, t, :],
                    pick[:],
                    vecs[:, GA_AT + t : GA_AT + t + 1],
                    b_pick[t][:, M_HALF * c : M_HALF * (c + 1)],
                    ALU.mult,
                    ALU.subtract,
                )

        pick_and_subtract([(0, 0), (0, 1)])
        pick_and_subtract([(1, 0), (1, 1)])
        pick_and_subtract([(2, 0), (3, 0)])
        nc.vector.quantize_mx(
            out=we_codes[:].bitcast(FP8X4), scales=we_scales[:], in_=we_bf[:].rearrange("p n t -> p (n t)")
        )
        pick_and_subtract([(2, 1), (3, 1)])

        out_rows = out.rearrange("(j p) m -> p j m", p=P)
        for c, interleave in enumerate((nc.scalar.copy, nc.vector.tensor_copy)):
            z_bf = sb([P, M_HALF, SLOTS], BF16, "z_bf%d" % c, "z_bf")
            interleave(z_bf[:], z_rows[c][:].rearrange("p t m -> p m t"))
            z_codes = sb([P, M_HALF], U32, "z_codes%d" % c)
            z_scales = sb([P, M_HALF], U8, "z_scales%d" % c)
            nc.vector.quantize_mx(
                out=z_codes[:].bitcast(FP8X4), scales=z_scales[:], in_=z_bf[:].rearrange("p m t -> p (m t)")
            )
            for j0 in range(0, OUT_TILES, 2):
                y_sb = sb([P, 2, M_HALF], F32, "y_sb%d%d" % (c, j0))
                for j in (j0, j0 + 1):
                    acc = bank(OUT_TILES * c + j)
                    nc.tensor.matmul_mx(
                        out=acc[:, 0:M_HALF],
                        lhsT=we_codes[:, j * P : (j + 1) * P].bitcast(FP8X4),
                        lhsT_scale=we_scales[:, j * P : (j + 1) * P],
                        rhs=z_codes[:].bitcast(FP8X4),
                        rhs_scale=z_scales[:],
                        start=True,
                        stop=True,
                    )
                    nc.scalar.activation(
                        y_sb[:, j - j0, :], acc[:, 0:M_HALF], ACT.Silu, bias=vecs[:, BE_AT + j : BE_AT + j + 1]
                    )
                nc.sync.dma_start(out_rows[:, j0 : j0 + 2, M_HALF * c : M_HALF * (c + 1)], y_sb[:])
